import numpy as np
import ml_dtypes


def mxq(x, axis, fmt="e4m3"):
    dtype, down = {"e4m3": (ml_dtypes.float8_e4m3fn, 7), "e5m2": (ml_dtypes.float8_e5m2, 14)}[fmt]
    v = np.moveaxis(np.asarray(x, np.float32).astype(ml_dtypes.bfloat16).astype(np.float64), axis, -1)
    blocks = v.reshape(v.shape[:-1] + (-1, 32))
    amax = np.abs(blocks).max(-1, keepdims=True)
    byte = np.maximum(np.where(amax > 0, np.frexp(amax)[1] - 1 + 127, 0) - down, 1)
    scale = np.exp2(byte - 127.0)
    codes = (blocks / scale).astype(np.float32).astype(dtype).astype(np.float64)
    return np.moveaxis((codes * scale).reshape(v.shape), -1, axis)


WIDE = False


def mx_kscale(k):
    if not WIDE:
        return np.ones(k)
    levels = np.array([10, -10, 5, -5, 0])
    if k % 512:
        return np.exp2(np.random.permutation(np.resize(levels, k // 32))).repeat(32)
    a = np.empty((k // 512, 16))
    for p in range(k // 512):
        a[p, :8] = np.random.permutation(np.resize(levels, 8))
        for g in range(8):
            far = levels[np.abs(levels - a[p, g]) >= 10]
            a[p, g + 8] = far[np.random.randint(len(far))]
    return np.exp2(a.ravel()).repeat(32)


def f64(x):
    return np.asarray(x).astype(np.float64)


def striped(idx):
    return np.tile(idx.reshape(-1, 16).T, (8, 1)).astype(np.uint16)


def unstriped(offs):
    return offs[:16].T.reshape(-1).astype(np.int64)


E2M1 = np.array([0.0, 0.5, 1.0, 1.5, 2.0, 3.0, 4.0, 6.0, -0.0, -0.5, -1.0, -1.5, -2.0, -3.0, -4.0, -6.0])


def pack_weight(w, fmt):
    k, n = w.shape
    w = f64(np.asarray(w, np.float32).astype(ml_dtypes.bfloat16)).reshape(k // 32, 32, n)
    amax = np.abs(w).max(1)
    if fmt == "e4m3":
        byte = np.frexp(amax)[1] - 1 + 127 - 7
    else:
        mant, ex = np.frexp(amax / 6.0)
        byte = np.where(mant > 0.5, ex, ex - 1) + 127
    byte = np.clip(np.where(amax > 0, byte, 1), 1, 254)
    scaled = (w * np.exp2(127.0 - byte)[:, None, :]).reshape(k, n).astype(np.float32)
    by_word = np.ascontiguousarray(scaled.reshape(k // 512, 128, 4, n).transpose(0, 1, 3, 2))
    if fmt == "e4m3":
        words = by_word.astype(ml_dtypes.float8_e4m3fn).view(np.uint8)
    else:
        c = by_word.astype(ml_dtypes.float4_e2m1fn).view(np.uint8) & 0xF
        words = (c[..., 0::2] | (c[..., 1::2] << 4)).reshape(k // 512, 128, 2 * n)
    return np.ascontiguousarray(words), np.ascontiguousarray(byte.astype(np.uint8).reshape(k // 512, 16, n))


def unpack_weight(words, scales, fmt):
    g, _, n = scales.shape
    words = np.ascontiguousarray(words).reshape(g, 128, n, -1)
    if fmt == "e4m3":
        vals = words.view(ml_dtypes.float8_e4m3fn).astype(np.float64)
    else:
        nib = np.empty((g, 128, n, 4), np.uint8)
        nib[..., 0::2] = words & 0xF
        nib[..., 1::2] = words >> 4
        vals = E2M1[nib]
    vals = vals * np.repeat(np.exp2(scales.astype(np.float64) - 127.0), 8, axis=1)[..., None]
    return vals.transpose(0, 1, 3, 2).reshape(g * 512, n)


def gelu(v):
    return 0.5 * v * (1.0 + np.tanh(np.sqrt(2.0 / np.pi) * (v + 0.044715 * v**3)))


K, H, N, T, S, T2 = 1024, 512, 384, 2048, 1024, 2048

def setup_inputs():
    n = np.random.standard_normal
    s = mx_kscale(K)[:, None]
    u = mx_kscale(H)[:, None]
    tab_words, tab_scales = pack_weight(n((K, T)) * s, "e4m3")
    wb_words, wb_scales = pack_weight(n((K, H)) * 0.92 / np.sqrt(K) / s, "e2m1")
    wg_words, wg_scales = pack_weight(n((K, H)) * 0.37 / np.sqrt(K) / s, "e2m1")
    wc_words, wc_scales = pack_weight(n((H, N)) * 1.5 / np.sqrt(H) / u, "e4m3")
    return {
        "tab_words": tab_words, "tab_scales": tab_scales,
        "offs": striped(np.random.permutation(T)[:S]),
        "offs2": striped(np.random.permutation(T)[:S]),
        "offs3": striped(np.random.permutation(T2)[:S]),
        "wa": (n((K, H)) * 0.92 / np.sqrt(K) / s).astype(np.float32),
        "wb_words": wb_words, "wb_scales": wb_scales,
        "wf": (n((K, H)) * 0.37 / np.sqrt(K) / s).astype(np.float32),
        "wg_words": wg_words, "wg_scales": wg_scales,
        "gain": (np.exp(0.3 * n(H)) * u[:, 0]).astype(np.float32),
        "wc_words": wc_words, "wc_scales": wc_scales,
        "road": (0.8 * n((N, S))).astype(np.float32),
        "wgo": np.exp(0.3 * n((128, S))).astype(np.float32),
    }

def reference(tab_words, tab_scales, offs, offs2, offs3, wa, wb_words, wb_scales, wf,
              wg_words, wg_scales, gain, wc_words, wc_scales, road, wgo):
    TW = unpack_weight(tab_words, tab_scales, "e4m3")
    v = TW[:, unstriped(offs)]
    v2 = TW[:, unstriped(offs2)]
    wb = unpack_weight(wb_words, wb_scales, "e2m1")
    wg = unpack_weight(wg_words, wg_scales, "e2m1")
    wc = unpack_weight(wc_words, wc_scales, "e4m3")
    e1 = mxq(f64(wa), 0, "e4m3").T @ v + wb.T @ v2
    e2 = mxq(f64(wf), 0, "e4m3").T @ v + wg.T @ v2
    h = f64(gain)[:, None] * (np.tanh(e1) * np.cos(e2))
    y = np.abs((wc.T @ mxq(h, 0, "e4m3")) + f64(road))
    out = np.zeros((N, T2))
    out[:, unstriped(offs3)] = np.tile(f64(wgo), (N // 128, 1)) * y
    return out

@@ -1,0 +1,272 @@
+from contextlib import ExitStack
+
+import concourse.mybir as mybir
+
+K, H, N, T, S, T2 = 1024, 512, 384, 2048, 1024, 2048
+FLOPS = 2 * (4 * K * H * S + H * N * S)
+
+F32 = mybir.dt.float32
+BF16 = mybir.dt.bfloat16
+I32 = mybir.dt.int32
+U32 = mybir.dt.uint32
+U16 = mybir.dt.uint16
+U8 = mybir.dt.uint8
+FP8X4 = mybir.dt.float8_e4m3fn_x4
+FP4X4 = mybir.dt.float4_e2m1fn_x4
+ACT = mybir.ActivationFunctionType
+ALU = mybir.AluOpType
+
+P = 128
+PACK = 4
+PASSES = K // (P * PACK)
+QUADRANTS = 4
+W = 256
+SLICES = S // W
+ROW_TILES = N // P
+SHIFT_ROWS = 112
+
+
+def tile_list_platoon_offer_features_kernel(
+    tc, tab_words, tab_scales, offs, offs2, offs3, wa, wb_words, wb_scales, wf,
+    wg_words, wg_scales, gain, wc_words, wc_scales, road, wgo, out,
+):
+    nc = tc.nc
+    with ExitStack() as ctx:
+        keep = ctx.enter_context(tc.tile_pool(name="keep", bufs=1))
+        picks = ctx.enter_context(tc.tile_pool(name="picks", bufs=3))
+        work = ctx.enter_context(tc.tile_pool(name="work", bufs=2))
+        psum1 = ctx.enter_context(tc.psum_pool(name="psum1", bufs=6))
+        psum2 = ctx.enter_context(tc.psum_pool(name="psum2", bufs=2))
+
+        def held(name, shape, dtype):
+            return keep.tile(shape, dtype, name=name, align_bytes=64)
+
+        lead_list = held("lead_list", [P, S // 16], U16)
+        join_list = held("join_list", [P, S // 16], U16)
+        offer_list = held("offer_list", [P, S // 16], U16)
+        table = [held("table%d" % a, [P, T], U32) for a in range(PASSES)]
+        table_scales = held("table_scales", [P, T], U8)
+        lead_scales = held("lead_scales", [P, S], U8)
+        join_scales = held("join_scales", [P, S], U8)
+        join_scales1 = held("join_scales1", [P, S], U8)
+        fp4_raw = [held("fp4_raw%d" % m, [P, PASSES, 2 * H], U8) for m in range(2)]
+        fp4 = [held("fp4_%d" % m, [P, PASSES, 2 * H], U8) for m in range(2)]
+        fp4_scales_raw = [held("fp4_scales_raw%d" % m, [P, PASSES, H], U8) for m in range(2)]
+        fp4_scales = [held("fp4_scales%d" % m, [P, PASSES, H], U8) for m in range(2)]
+        w_raw = [[held("w_raw%d%d" % (m, a), [P, PACK, H], F32) for a in range(PASSES)] for m in range(2)]
+        w_bf = [[held("w_bf%d%d" % (m, a), [P, PACK * H], BF16) for a in range(PASSES)] for m in range(2)]
+        w_codes = [[held("w_codes%d%d" % (m, a), [P, H], U32) for a in range(PASSES)] for m in range(2)]
+        w_scales = [[held("w_scales%d%d" % (m, a), [P, H], U8) for a in range(PASSES)] for m in range(2)]
+        wc_codes = held("wc_codes", [P, N], U32)
+        wc_plane = held("wc_plane", [P, 1, N], U8)
+        gain_sb = held("gain_sb", [P, PACK], F32)
+        gain_m2 = held("gain_m2", [P, PACK], F32)
+        wgo_sb = held("wgo_sb", [P, S], F32)
+        road_sb = [held("road%d" % s, [P, ROW_TILES, W], F32) for s in range(SLICES)]
+        pages = [held("page%d" % n, [P, T2], F32) for n in range(ROW_TILES)]
+
+        nc.gpsimd.memset(table_scales[:].bitcast(I32), 0)
+        for plane in (fp4_scales_raw[1], fp4_scales_raw[0], join_scales1, wc_plane):
+            nc.vector.memset(plane[:].bitcast(I32), 0)
+        for page in pages:
+            nc.gpsimd.memset(page[:], 0.0)
+        warm = held("warm", [P, 2], F32)
+        nc.vector.memset(warm[:, 0:1], 0.0)
+        nc.scalar.activation(out=warm[:, 1:2], in_=warm[:, 0:1], func=ACT.Silu)
+
+        def load_table(a):
+            nc.sync.dma_start(
+                out=table[a][:].bitcast(I32),
+                in_=tab_words[a].rearrange("p t i -> p (t i)").bitcast(I32),
+            )
+
+        def load_table_scales():
+            for q in range(QUADRANTS):
+                nc.sync.dma_start(
+                    out=table_scales[32 * q : 32 * q + 4 * PASSES, :].bitcast(I32),
+                    in_=tab_scales[:, 4 * q : 4 * q + 4, :].bitcast(I32),
+                )
+
+        def load_scale_rows(plane, scales):
+            for q in range(QUADRANTS):
+                nc.sync.dma_start(
+                    out=plane[32 * q : 32 * q + 4].bitcast(I32),
+                    in_=scales[:, 4 * q : 4 * q + 4, :].rearrange("a r c -> r a c").bitcast(I32),
+                )
+
+        def load_fp4(m, words):
+            nc.sync.dma_start(
+                out=fp4_raw[m][:].bitcast(I32),
+                in_=words.rearrange("a p c -> p a c").bitcast(I32),
+            )
+
+        def load_weight(m, a, w):
+            nc.sync.dma_start(
+                out=w_raw[m][a][:],
+                in_=w[512 * a : 512 * (a + 1), :].rearrange("(p j) c -> p j c", j=PACK),
+            )
+
+        nc.sync.dma_start(join_list[:], offs2)
+        nc.sync.dma_start(lead_list[:], offs)
+        load_table_scales()
+        load_weight(1, 0, wf)
+        load_fp4(1, wg_words)
+        load_table(0)
+        load_scale_rows(fp4_scales_raw[1], wg_scales)
+        load_weight(0, 0, wa)
+        load_scale_rows(fp4_scales_raw[0], wb_scales)
+        nc.sync.dma_start(out=gain_sb[:], in_=gain.rearrange("(p t) -> p t", t=PACK))
+        load_weight(1, 1, wf)
+        load_fp4(0, wb_words)
+        load_table(1)
+        load_weight(0, 1, wa)
+        nc.sync.dma_start(
+            out=wc_codes[:].bitcast(I32),
+            in_=wc_words[0].rearrange("p c i -> p (c i)").bitcast(I32),
+        )
+        load_scale_rows(wc_plane, wc_scales)
+        road_rows = road.rearrange("(n p) j -> p n j", p=P)
+        nc.sync.dma_start(out=road_sb[0][:], in_=road_rows[:, :, 0:W])
+        nc.sync.dma_start(offer_list[:], offs3)
+        nc.sync.dma_start(out=wgo_sb[:], in_=wgo)
+        for s in range(1, SLICES):
+            nc.sync.dma_start(out=road_sb[s][:], in_=road_rows[:, :, s * W : (s + 1) * W])
+
+        nc.vector.tensor_copy(out=join_scales[:], in_=table_scales[:].indirect(join_list[:]))
+        nc.gpsimd.dma_start(
+            out=join_scales1[0:SHIFT_ROWS, :].bitcast(I32),
+            in_=join_scales[4 : 4 + SHIFT_ROWS, :].bitcast(I32),
+        )
+        nc.vector.tensor_copy(out=lead_scales[:], in_=table_scales[:].indirect(lead_list[:]))
+        for m in (1, 0):
+            nc.gpsimd.tensor_copy(
+                out=fp4_scales[m][:].rearrange("p a (t m) -> p a t m", t=PACK),
+                in_=fp4_scales_raw[m][:].rearrange("p a (m t) -> p a t m", t=PACK),
+            )
+
+        for m in (1, 0):
+            nc.scalar.copy(
+                out=fp4[m][:].bitcast(U16).rearrange("p a (t m) -> p a t m", t=PACK),
+                in_=fp4_raw[m][:].bitcast(U16).rearrange("p a (m t) -> p a t m", t=PACK),
+            )
+        nc.scalar.activation(out=gain_m2[:], in_=gain_sb[:], func=ACT.Copy, scale=-2.0)
+
+        for a in range(PASSES):
+            for m in (1, 0):
+                dst = w_bf[m][a][:].rearrange("p (t m j) -> p m j t", t=PACK, j=PACK)
+                src = w_raw[m][a][:].rearrange("p j (m t) -> p m j t", t=PACK)
+                if (m, a) == (0, 1):
+                    nc.vector.tensor_copy(out=dst, in_=src)
+                else:
+                    nc.scalar.copy(out=dst, in_=src)
+                nc.vector.quantize_mx(
+                    out=w_codes[m][a][:].bitcast(FP8X4), scales=w_scales[m][a][:], in_=w_bf[m][a][:]
+                )
+
+        join_planes = [join_scales, join_scales1]
+
+        def gather_words(s):
+            picked = {}
+            for a in range(PASSES):
+                for name, lst in (("lead", lead_list), ("join", join_list)):
+                    words = picks.tile([P, W], U32, name="%s%d" % (name, a), align_bytes=64, bufs=SLICES - 2 * a)
+                    nc.vector.tensor_copy(
+                        out=words[:], in_=table[a][:].indirect(lst[:, s * W // 16 : (s + 1) * W // 16])
+                    )
+                    picked[name, a] = words
+            return picked
+
+        def first_stage_bank(m, pair, picked, cols):
+            bank = psum1.tile([P, 2, W], F32, name="sums")
+            steps = [(name, a) for a in range(PASSES) for name in ("join", "lead")]
+            for i, (name, a) in enumerate(steps):
+                for u in range(2):
+                    t = 2 * pair + u
+                    if name == "join":
+                        lhs = fp4[m][:, a, 2 * P * t : 2 * P * (t + 1)].bitcast(FP4X4)
+                        lhs_scale = fp4_scales[m][:, a, P * t : P * (t + 1)]
+                        rhs_scale = join_planes[a][:, cols]
+                    else:
+                        lhs = w_codes[m][a][:, P * t : P * (t + 1)].bitcast(FP8X4)
+                        lhs_scale = w_scales[m][a][:, P * t : P * (t + 1)]
+                        rhs_scale = lead_scales[4 * a : P, cols]
+                    nc.tensor.matmul_mx(
+                        out=bank[:, u, :], lhsT=lhs, lhsT_scale=lhs_scale,
+                        rhs=picked[name, a][:].bitcast(FP8X4), rhs_scale=rhs_scale,
+                        start=(i == 0 and u == 0), stop=(i == len(steps) - 1 and u == 1),
+                    )
+            return bank
+
+        def place(n, values, first, count):
+            nc.vector.tensor_tensor(
+                out=pages[n][:].indirect(offer_list[:, first // 16 : (first + count) // 16]),
+                in0=values, in1=wgo_sb[:, first : first + count], op=ALU.mult,
+            )
+
+        for s in range(SLICES):
+            cols = slice(s * W, (s + 1) * W)
+            picked = gather_words(s)
+            half_sin = work.tile([P, PACK, W], F32)
+            sin_sq = work.tile([P, PACK, W], F32)
+            gain_cos = work.tile([P, PACK, W], F32)
+            tanh = work.tile([P, PACK, W], F32)
+            for pair in range(2):
+                e2 = first_stage_bank(1, pair, picked, cols)
+                both = slice(2 * pair, 2 * pair + 2)
+                nc.scalar.activation(out=half_sin[:, both, :], in_=e2[:], func=ACT.Sin, scale=0.5)
+                nc.scalar.activation(out=sin_sq[:, both, :], in_=half_sin[:, both, :], func=ACT.Square)
+                for t in range(2 * pair, 2 * pair + 2):
+                    nc.scalar.activation(
+                        out=gain_cos[:, t, :], in_=sin_sq[:, t, :], func=ACT.Identity,
+                        scale=gain_m2[:, t : t + 1], bias=gain_sb[:, t : t + 1],
+                    )
+            for pair in range(2):
+                e1 = first_stage_bank(0, pair, picked, cols)
+                nc.scalar.activation(out=tanh[:, 2 * pair : 2 * pair + 2, :], in_=e1[:], func=ACT.Tanh)
+
+            h_bf = work.tile([P, PACK * W], BF16, align_bytes=64)
+            nc.vector.tensor_tensor(
+                out=h_bf[:].rearrange("p (c i t) -> p c t i", i=4, t=PACK),
+                in0=gain_cos[:].rearrange("p t (c i) -> p c t i", i=4),
+                in1=tanh[:].rearrange("p t (c i) -> p c t i", i=4),
+                op=ALU.mult,
+            )
+            last = s == SLICES - 1
+            if last:
+                spots = [gain_cos[:, 0, :], tanh[:, 0, :], tanh[:, 2, :]]
+            else:
+                spots = [tanh[:, n, :] for n in range(ROW_TILES)]
+            if s > 0:
+                for n in range(ROW_TILES):
+                    nc.scalar.activation(out=spots[n], in_=shifted[:, n, :], func=ACT.Abs)
+            h_codes = work.tile([P, W], U32, align_bytes=64)
+            h_scales = work.tile([P, W], U8, align_bytes=64)
+            nc.vector.quantize_mx(out=h_codes[:].bitcast(FP8X4), scales=h_scales[:], in_=h_bf[:])
+            if s > 0:
+                for n in range(1 if last else ROW_TILES):
+                    place(n, spots[n], (s - 1) * W, W)
+
+            shifted = work.tile([P, ROW_TILES, W], F32)
+            for n0, n1 in ((0, 2), (2, 3)):
+                bank = psum2.tile([P, 2, W], F32, name="second")
+                for n in range(n0, n1):
+                    nc.tensor.matmul_mx(
+                        out=bank[:, n - n0, :],
+                        lhsT=wc_codes[:, P * n : P * (n + 1)].bitcast(FP8X4),
+                        lhsT_scale=wc_plane[:, 0, P * n : P * (n + 1)],
+                        rhs=h_codes[:].bitcast(FP8X4), rhs_scale=h_scales[:],
+                        start=True, stop=True,
+                    )
+                nc.vector.tensor_tensor(
+                    out=shifted[:, n0:n1, :], in0=bank[:, 0 : n1 - n0, :], in1=road_sb[s][:, n0:n1, :], op=ALU.add
+                )
+
+        spots = [gain_cos[:, 1, :], tanh[:, 1, :], tanh[:, 3, :]]
+        for n in range(ROW_TILES):
+            nc.scalar.activation(out=spots[n], in_=shifted[:, n, :], func=ACT.Abs)
+        place(0, spots[0], S - W, W)
+        for n in range(1, ROW_TILES):
+            place(n, tanh[:, 2 * n - 2 : 2 * n, :].rearrange("p u j -> p (u j)"), S - 2 * W, 2 * W)
+
+        for n in range(ROW_TILES):
+            nc.sync.dma_start(out=out[P * n : P * (n + 1), :], in_=pages[n][:])

@@ -65,14 +65,14 @@ def tile_list_platoon_offer_features_kernel(
         road_sb = [held("road%d" % s, [P, ROW_TILES, W], F32) for s in range(SLICES)]
         pages = [held("page%d" % n, [P, T2], F32) for n in range(ROW_TILES)]
 
-        nc.gpsimd.memset(table_scales[:].bitcast(I32), 0)
+        warm = held("warm", [P, 2], F32)
+        nc.vector.memset(table_scales[:].bitcast(I32), 0)
+        nc.vector.memset(warm[:, 0:1], 0.0)
+        nc.scalar.activation(out=warm[:, 1:2], in_=warm[:, 0:1], func=ACT.Silu)
         for plane in (fp4_scales_raw[1], fp4_scales_raw[0], join_scales1, wc_plane):
             nc.vector.memset(plane[:].bitcast(I32), 0)
         for page in pages:
-            nc.gpsimd.memset(page[:], 0.0)
-        warm = held("warm", [P, 2], F32)
-        nc.vector.memset(warm[:, 0:1], 0.0)
-        nc.scalar.activation(out=warm[:, 1:2], in_=warm[:, 0:1], func=ACT.Silu)
+            nc.vector.memset(page[:], 0.0)
 
         def load_table(a):
             nc.sync.dma_start(
@@ -139,7 +139,7 @@ def tile_list_platoon_offer_features_kernel(
         )
         nc.vector.tensor_copy(out=lead_scales[:], in_=table_scales[:].indirect(lead_list[:]))
         for m in (1, 0):
-            nc.gpsimd.tensor_copy(
+            nc.vector.tensor_copy(
                 out=fp4_scales[m][:].rearrange("p a (t m) -> p a t m", t=PACK),
                 in_=fp4_scales_raw[m][:].rearrange("p a (m t) -> p a t m", t=PACK),
             )
@@ -169,7 +169,7 @@ def tile_list_platoon_offer_features_kernel(
             picked = {}
             for a in range(PASSES):
                 for name, lst in (("lead", lead_list), ("join", join_list)):
-                    words = picks.tile([P, W], U32, name="%s%d" % (name, a), align_bytes=64, bufs=SLICES - 2 * a)
+                    words = picks.tile([P, W], U32, name="%s%d" % (name, a), align_bytes=64, bufs=3 - a)
                     nc.vector.tensor_copy(
                         out=words[:], in_=table[a][:].indirect(lst[:, s * W // 16 : (s + 1) * W // 16])
                     )

@@ -71,8 +71,6 @@ def tile_list_platoon_offer_features_kernel(
         nc.scalar.activation(out=warm[:, 1:2], in_=warm[:, 0:1], func=ACT.Silu)
         for plane in (fp4_scales_raw[1], fp4_scales_raw[0], join_scales1, wc_plane):
             nc.vector.memset(plane[:].bitcast(I32), 0)
-        for page in pages:
-            nc.vector.memset(page[:], 0.0)
 
         def load_table(a):
             nc.sync.dma_start(
@@ -109,16 +107,21 @@ def tile_list_platoon_offer_features_kernel(
         nc.sync.dma_start(join_list[:], offs2)
         nc.sync.dma_start(lead_list[:], offs)
         load_table_scales()
+        nc.vector.tensor_copy(out=join_scales[:], in_=table_scales[:].indirect(join_list[:]))
         load_weight(1, 0, wf)
         load_fp4(1, wg_words)
         load_table(0)
         load_scale_rows(fp4_scales_raw[1], wg_scales)
         load_weight(0, 0, wa)
-        load_scale_rows(fp4_scales_raw[0], wb_scales)
-        nc.sync.dma_start(out=gain_sb[:], in_=gain.rearrange("(p t) -> p t", t=PACK))
+        nc.sync.dma_start(
+            out=join_scales1[0:SHIFT_ROWS, :].bitcast(I32),
+            in_=join_scales[4 : 4 + SHIFT_ROWS, :].bitcast(I32),
+        )
         load_weight(1, 1, wf)
-        load_fp4(0, wb_words)
+        nc.sync.dma_start(out=gain_sb[:], in_=gain.rearrange("(p t) -> p t", t=PACK))
         load_table(1)
+        load_fp4(0, wb_words)
+        load_scale_rows(fp4_scales_raw[0], wb_scales)
         load_weight(0, 1, wa)
         nc.sync.dma_start(
             out=wc_codes[:].bitcast(I32),
@@ -132,12 +135,9 @@ def tile_list_platoon_offer_features_kernel(
         for s in range(1, SLICES):
             nc.sync.dma_start(out=road_sb[s][:], in_=road_rows[:, :, s * W : (s + 1) * W])
 
-        nc.vector.tensor_copy(out=join_scales[:], in_=table_scales[:].indirect(join_list[:]))
-        nc.gpsimd.dma_start(
-            out=join_scales1[0:SHIFT_ROWS, :].bitcast(I32),
-            in_=join_scales[4 : 4 + SHIFT_ROWS, :].bitcast(I32),
-        )
         nc.vector.tensor_copy(out=lead_scales[:], in_=table_scales[:].indirect(lead_list[:]))
+        for page in pages:
+            nc.vector.memset(page[:].bitcast(I32), 0)
         for m in (1, 0):
             nc.vector.tensor_copy(
                 out=fp4_scales[m][:].rearrange("p a (t m) -> p a t m", t=PACK),
@@ -169,14 +169,15 @@ def tile_list_platoon_offer_features_kernel(
             picked = {}
             for a in range(PASSES):
                 for name, lst in (("lead", lead_list), ("join", join_list)):
-                    words = picks.tile([P, W], U32, name="%s%d" % (name, a), align_bytes=64, bufs=3 - a)
+                    words = picks.tile([P, W], U32, name="%s%d" % (name, a), align_bytes=64, bufs=SLICES - 2 * a)
                     nc.vector.tensor_copy(
                         out=words[:], in_=table[a][:].indirect(lst[:, s * W // 16 : (s + 1) * W // 16])
                     )
                     picked[name, a] = words
             return picked
 
-        def first_stage_bank(m, pair, picked, cols):
+        def first_stage_bank(m, pair, picked, s):
+            cols = slice(s * W, (s + 1) * W)
             bank = psum1.tile([P, 2, W], F32, name="sums")
             steps = [(name, a) for a in range(PASSES) for name in ("join", "lead")]
             for i, (name, a) in enumerate(steps):
@@ -203,32 +204,51 @@ def tile_list_platoon_offer_features_kernel(
                 in0=values, in1=wgo_sb[:, first : first + count], op=ALU.mult,
             )
 
+        def second_stage(s, h_codes, h_scales):
+            shifted = work.tile([P, ROW_TILES, W], F32)
+            for n0, n1 in ((0, 2), (2, 3)):
+                bank = psum2.tile([P, 2, W], F32, name="second")
+                for n in range(n0, n1):
+                    nc.tensor.matmul_mx(
+                        out=bank[:, n - n0, :],
+                        lhsT=wc_codes[:, P * n : P * (n + 1)].bitcast(FP8X4),
+                        lhsT_scale=wc_plane[:, 0, P * n : P * (n + 1)],
+                        rhs=h_codes[:].bitcast(FP8X4), rhs_scale=h_scales[:],
+                        start=True, stop=True,
+                    )
+                nc.vector.tensor_tensor(
+                    out=shifted[:, n0:n1, :], in0=bank[:, 0 : n1 - n0, :], in1=road_sb[s][:, n0:n1, :], op=ALU.add
+                )
+            return shifted
+
         for s in range(SLICES):
-            cols = slice(s * W, (s + 1) * W)
             picked = gather_words(s)
             half_sin = work.tile([P, PACK, W], F32)
             sin_sq = work.tile([P, PACK, W], F32)
             gain_cos = work.tile([P, PACK, W], F32)
-            tanh = work.tile([P, PACK, W], F32)
+            tanh = work.tile([P, PACK, W], F32, bufs=3)
             for pair in range(2):
-                e2 = first_stage_bank(1, pair, picked, cols)
+                e2 = first_stage_bank(1, pair, picked, s)
+                nc.scalar.activation(out=half_sin[:, 2 * pair : 2 * pair + 2, :], in_=e2[:], func=ACT.Sin, scale=0.5)
+            for pair in range(2):
                 both = slice(2 * pair, 2 * pair + 2)
-                nc.scalar.activation(out=half_sin[:, both, :], in_=e2[:], func=ACT.Sin, scale=0.5)
                 nc.scalar.activation(out=sin_sq[:, both, :], in_=half_sin[:, both, :], func=ACT.Square)
-                for t in range(2 * pair, 2 * pair + 2):
-                    nc.scalar.activation(
-                        out=gain_cos[:, t, :], in_=sin_sq[:, t, :], func=ACT.Identity,
-                        scale=gain_m2[:, t : t + 1], bias=gain_sb[:, t : t + 1],
-                    )
+            for t in range(PACK):
+                nc.scalar.activation(
+                    out=gain_cos[:, t, :], in_=sin_sq[:, t, :], func=ACT.Identity,
+                    scale=gain_m2[:, t : t + 1], bias=gain_sb[:, t : t + 1],
+                )
             for pair in range(2):
-                e1 = first_stage_bank(0, pair, picked, cols)
+                e1 = first_stage_bank(0, pair, picked, s)
                 nc.scalar.activation(out=tanh[:, 2 * pair : 2 * pair + 2, :], in_=e1[:], func=ACT.Tanh)
+            if s > 0:
+                shifted = second_stage(s - 1, h_codes, h_scales)
 
             h_bf = work.tile([P, PACK * W], BF16, align_bytes=64)
             nc.vector.tensor_tensor(
-                out=h_bf[:].rearrange("p (c i t) -> p c t i", i=4, t=PACK),
-                in0=gain_cos[:].rearrange("p t (c i) -> p c t i", i=4),
-                in1=tanh[:].rearrange("p t (c i) -> p c t i", i=4),
+                out=h_bf[:].rearrange("p (c i t) -> p c t i", i=2, t=PACK),
+                in0=gain_cos[:].rearrange("p t (c i) -> p c t i", i=2),
+                in1=tanh[:].rearrange("p t (c i) -> p c t i", i=2),
                 op=ALU.mult,
             )
             last = s == SLICES - 1
@@ -246,21 +266,7 @@ def tile_list_platoon_offer_features_kernel(
                 for n in range(1 if last else ROW_TILES):
                     place(n, spots[n], (s - 1) * W, W)
 
-            shifted = work.tile([P, ROW_TILES, W], F32)
-            for n0, n1 in ((0, 2), (2, 3)):
-                bank = psum2.tile([P, 2, W], F32, name="second")
-                for n in range(n0, n1):
-                    nc.tensor.matmul_mx(
-                        out=bank[:, n - n0, :],
-                        lhsT=wc_codes[:, P * n : P * (n + 1)].bitcast(FP8X4),
-                        lhsT_scale=wc_plane[:, 0, P * n : P * (n + 1)],
-                        rhs=h_codes[:].bitcast(FP8X4), rhs_scale=h_scales[:],
-                        start=True, stop=True,
-                    )
-                nc.vector.tensor_tensor(
-                    out=shifted[:, n0:n1, :], in0=bank[:, 0 : n1 - n0, :], in1=road_sb[s][:, n0:n1, :], op=ALU.add
-                )
-
+        shifted = second_stage(SLICES - 1, h_codes, h_scales)
         spots = [gain_cos[:, 1, :], tanh[:, 1, :], tanh[:, 3, :]]
         for n in range(ROW_TILES):
             nc.scalar.activation(out=spots[n], in_=shifted[:, n, :], func=ACT.Abs)

@@ -153,15 +153,20 @@ def tile_list_platoon_offer_features_kernel(
 
         for a in range(PASSES):
             for m in (1, 0):
-                dst = w_bf[m][a][:].rearrange("p (t m j) -> p m j t", t=PACK, j=PACK)
-                src = w_raw[m][a][:].rearrange("p j (m t) -> p m j t", t=PACK)
-                if (m, a) == (0, 1):
-                    nc.vector.tensor_copy(out=dst, in_=src)
-                else:
-                    nc.scalar.copy(out=dst, in_=src)
-                nc.vector.quantize_mx(
-                    out=w_codes[m][a][:].bitcast(FP8X4), scales=w_scales[m][a][:], in_=w_bf[m][a][:]
-                )
+                dst = w_bf[m][a][:].rearrange("p (pair u c i j) -> p pair c j i u", pair=2, u=2, i=2, j=PACK)
+                src = w_raw[m][a][:].rearrange("p j (c i pair u) -> p pair c j i u", pair=2, u=2, i=2)
+                for pair in range(2):
+                    if (m, a) == (0, 1):
+                        nc.vector.tensor_copy(out=dst[:, pair], in_=src[:, pair])
+                    else:
+                        nc.scalar.copy(out=dst[:, pair], in_=src[:, pair])
+                for pair in range(2):
+                    half = slice(2 * P * pair, 2 * P * (pair + 1))
+                    nc.vector.quantize_mx(
+                        out=w_codes[m][a][:, half].bitcast(FP8X4),
+                        scales=w_scales[m][a][:, half],
+                        in_=w_bf[m][a][:, 2 * H * pair : 2 * H * (pair + 1)],
+                    )
 
         join_planes = [join_scales, join_scales1]
 

from contextlib import ExitStack

import concourse.mybir as mybir

K, H, N, T, S, T2 = 1024, 512, 384, 2048, 1024, 2048
FLOPS = 2 * (4 * K * H * S + H * N * S)

F32 = mybir.dt.float32
BF16 = mybir.dt.bfloat16
I32 = mybir.dt.int32
U32 = mybir.dt.uint32
U16 = mybir.dt.uint16
U8 = mybir.dt.uint8
FP8X4 = mybir.dt.float8_e4m3fn_x4
FP4X4 = mybir.dt.float4_e2m1fn_x4
ACT = mybir.ActivationFunctionType
ALU = mybir.AluOpType

P = 128
PACK = 4
PASSES = K // (P * PACK)
QUADRANTS = 4
W = 256
SLICES = S // W
ROW_TILES = N // P
SHIFT_ROWS = 112


def tile_list_platoon_offer_features_kernel(
    tc, tab_words, tab_scales, offs, offs2, offs3, wa, wb_words, wb_scales, wf,
    wg_words, wg_scales, gain, wc_words, wc_scales, road, wgo, out,
):
    nc = tc.nc
    with ExitStack() as ctx:
        keep = ctx.enter_context(tc.tile_pool(name="keep", bufs=1))
        picks = ctx.enter_context(tc.tile_pool(name="picks", bufs=3))
        work = ctx.enter_context(tc.tile_pool(name="work", bufs=2))
        psum1 = ctx.enter_context(tc.psum_pool(name="psum1", bufs=6))
        psum2 = ctx.enter_context(tc.psum_pool(name="psum2", bufs=2))

        def held(name, shape, dtype):
            return keep.tile(shape, dtype, name=name, align_bytes=64)

        lead_list = held("lead_list", [P, S // 16], U16)
        join_list = held("join_list", [P, S // 16], U16)
        offer_list = held("offer_list", [P, S // 16], U16)
        table = [held("table%d" % a, [P, T], U32) for a in range(PASSES)]
        table_scales = held("table_scales", [P, T], U8)
        lead_scales = held("lead_scales", [P, S], U8)
        join_scales = held("join_scales", [P, S], U8)
        join_scales1 = held("join_scales1", [P, S], U8)
        fp4_raw = [held("fp4_raw%d" % m, [P, PASSES, 2 * H], U8) for m in range(2)]
        fp4 = [held("fp4_%d" % m, [P, PASSES, 2 * H], U8) for m in range(2)]
        fp4_scales_raw = [held("fp4_scales_raw%d" % m, [P, PASSES, H], U8) for m in range(2)]
        fp4_scales = [held("fp4_scales%d" % m, [P, PASSES, H], U8) for m in range(2)]
        w_raw = [[held("w_raw%d%d" % (m, a), [P, PACK, H], F32) for a in range(PASSES)] for m in range(2)]
        w_bf = [[held("w_bf%d%d" % (m, a), [P, PACK * H], BF16) for a in range(PASSES)] for m in range(2)]
        w_codes = [[held("w_codes%d%d" % (m, a), [P, H], U32) for a in range(PASSES)] for m in range(2)]
        w_scales = [[held("w_scales%d%d" % (m, a), [P, H], U8) for a in range(PASSES)] for m in range(2)]
        wc_codes = held("wc_codes", [P, N], U32)
        wc_plane = held("wc_plane", [P, 1, N], U8)
        gain_sb = held("gain_sb", [P, PACK], F32)
        gain_m2 = held("gain_m2", [P, PACK], F32)
        wgo_sb = held("wgo_sb", [P, S], F32)
        road_sb = [held("road%d" % s, [P, ROW_TILES, W], F32) for s in range(SLICES)]
        pages = [held("page%d" % n, [P, T2], F32) for n in range(ROW_TILES)]

        warm = held("warm", [P, 2], F32)
        nc.vector.memset(table_scales[:].bitcast(I32), 0)
        nc.vector.memset(warm[:, 0:1], 0.0)
        nc.scalar.activation(out=warm[:, 1:2], in_=warm[:, 0:1], func=ACT.Silu)
        for plane in (fp4_scales_raw[1], fp4_scales_raw[0], join_scales1, wc_plane):
            nc.vector.memset(plane[:].bitcast(I32), 0)

        def load_table(a):
            nc.sync.dma_start(
                out=table[a][:].bitcast(I32),
                in_=tab_words[a].rearrange("p t i -> p (t i)").bitcast(I32),
            )

        def load_table_scales():
            for q in range(QUADRANTS):
                nc.sync.dma_start(
                    out=table_scales[32 * q : 32 * q + 4 * PASSES, :].bitcast(I32),
                    in_=tab_scales[:, 4 * q : 4 * q + 4, :].bitcast(I32),
                )

        def load_scale_rows(plane, scales):
            for q in range(QUADRANTS):
                nc.sync.dma_start(
                    out=plane[32 * q : 32 * q + 4].bitcast(I32),
                    in_=scales[:, 4 * q : 4 * q + 4, :].rearrange("a r c -> r a c").bitcast(I32),
                )

        def load_fp4(m, words):
            nc.sync.dma_start(
                out=fp4_raw[m][:].bitcast(I32),
                in_=words.rearrange("a p c -> p a c").bitcast(I32),
            )

        def load_weight(m, a, w):
            nc.sync.dma_start(
                out=w_raw[m][a][:],
                in_=w[512 * a : 512 * (a + 1), :].rearrange("(p j) c -> p j c", j=PACK),
            )

        nc.sync.dma_start(join_list[:], offs2)
        nc.sync.dma_start(lead_list[:], offs)
        load_table_scales()
        nc.vector.tensor_copy(out=join_scales[:], in_=table_scales[:].indirect(join_list[:]))
        load_weight(1, 0, wf)
        load_fp4(1, wg_words)
        load_table(0)
        load_scale_rows(fp4_scales_raw[1], wg_scales)
        load_weight(0, 0, wa)
        nc.sync.dma_start(
            out=join_scales1[0:SHIFT_ROWS, :].bitcast(I32),
            in_=join_scales[4 : 4 + SHIFT_ROWS, :].bitcast(I32),
        )
        load_weight(1, 1, wf)
        nc.sync.dma_start(out=gain_sb[:], in_=gain.rearrange("(p t) -> p t", t=PACK))
        load_table(1)
        load_fp4(0, wb_words)
        load_scale_rows(fp4_scales_raw[0], wb_scales)
        load_weight(0, 1, wa)
        nc.sync.dma_start(
            out=wc_codes[:].bitcast(I32),
            in_=wc_words[0].rearrange("p c i -> p (c i)").bitcast(I32),
        )
        load_scale_rows(wc_plane, wc_scales)
        road_rows = road.rearrange("(n p) j -> p n j", p=P)
        nc.sync.dma_start(out=road_sb[0][:], in_=road_rows[:, :, 0:W])
        nc.sync.dma_start(offer_list[:], offs3)
        nc.sync.dma_start(out=wgo_sb[:], in_=wgo)
        for s in range(1, SLICES):
            nc.sync.dma_start(out=road_sb[s][:], in_=road_rows[:, :, s * W : (s + 1) * W])

        nc.vector.tensor_copy(out=lead_scales[:], in_=table_scales[:].indirect(lead_list[:]))
        for page in pages:
            nc.vector.memset(page[:].bitcast(I32), 0)
        for m in (1, 0):
            nc.vector.tensor_copy(
                out=fp4_scales[m][:].rearrange("p a (t m) -> p a t m", t=PACK),
                in_=fp4_scales_raw[m][:].rearrange("p a (m t) -> p a t m", t=PACK),
            )

        for m in (1, 0):
            nc.scalar.copy(
                out=fp4[m][:].bitcast(U16).rearrange("p a (t m) -> p a t m", t=PACK),
                in_=fp4_raw[m][:].bitcast(U16).rearrange("p a (m t) -> p a t m", t=PACK),
            )
        nc.scalar.activation(out=gain_m2[:], in_=gain_sb[:], func=ACT.Copy, scale=-2.0)

        for a in range(PASSES):
            for m in (1, 0):
                dst = w_bf[m][a][:].rearrange("p (pair u c i j) -> p pair c j i u", pair=2, u=2, i=2, j=PACK)
                src = w_raw[m][a][:].rearrange("p j (c i pair u) -> p pair c j i u", pair=2, u=2, i=2)
                for pair in range(2):
                    if (m, a) == (0, 1):
                        nc.vector.tensor_copy(out=dst[:, pair], in_=src[:, pair])
                    else:
                        nc.scalar.copy(out=dst[:, pair], in_=src[:, pair])
                for pair in range(2):
                    half = slice(2 * P * pair, 2 * P * (pair + 1))
                    nc.vector.quantize_mx(
                        out=w_codes[m][a][:, half].bitcast(FP8X4),
                        scales=w_scales[m][a][:, half],
                        in_=w_bf[m][a][:, 2 * H * pair : 2 * H * (pair + 1)],
                    )

        join_planes = [join_scales, join_scales1]

        def gather_words(s):
            picked = {}
            for a in range(PASSES):
                for name, lst in (("lead", lead_list), ("join", join_list)):
                    words = picks.tile([P, W], U32, name="%s%d" % (name, a), align_bytes=64, bufs=SLICES - 2 * a)
                    nc.vector.tensor_copy(
                        out=words[:], in_=table[a][:].indirect(lst[:, s * W // 16 : (s + 1) * W // 16])
                    )
                    picked[name, a] = words
            return picked

        def first_stage_bank(m, pair, picked, s):
            cols = slice(s * W, (s + 1) * W)
            bank = psum1.tile([P, 2, W], F32, name="sums")
            steps = [(name, a) for a in range(PASSES) for name in ("join", "lead")]
            for i, (name, a) in enumerate(steps):
                for u in range(2):
                    t = 2 * pair + u
                    if name == "join":
                        lhs = fp4[m][:, a, 2 * P * t : 2 * P * (t + 1)].bitcast(FP4X4)
                        lhs_scale = fp4_scales[m][:, a, P * t : P * (t + 1)]
                        rhs_scale = join_planes[a][:, cols]
                    else:
                        lhs = w_codes[m][a][:, P * t : P * (t + 1)].bitcast(FP8X4)
                        lhs_scale = w_scales[m][a][:, P * t : P * (t + 1)]
                        rhs_scale = lead_scales[4 * a : P, cols]
                    nc.tensor.matmul_mx(
                        out=bank[:, u, :], lhsT=lhs, lhsT_scale=lhs_scale,
                        rhs=picked[name, a][:].bitcast(FP8X4), rhs_scale=rhs_scale,
                        start=(i == 0 and u == 0), stop=(i == len(steps) - 1 and u == 1),
                    )
            return bank

        def place(n, values, first, count):
            nc.vector.tensor_tensor(
                out=pages[n][:].indirect(offer_list[:, first // 16 : (first + count) // 16]),
                in0=values, in1=wgo_sb[:, first : first + count], op=ALU.mult,
            )

        def second_stage(s, h_codes, h_scales):
            shifted = work.tile([P, ROW_TILES, W], F32)
            for n0, n1 in ((0, 2), (2, 3)):
                bank = psum2.tile([P, 2, W], F32, name="second")
                for n in range(n0, n1):
                    nc.tensor.matmul_mx(
                        out=bank[:, n - n0, :],
                        lhsT=wc_codes[:, P * n : P * (n + 1)].bitcast(FP8X4),
                        lhsT_scale=wc_plane[:, 0, P * n : P * (n + 1)],
                        rhs=h_codes[:].bitcast(FP8X4), rhs_scale=h_scales[:],
                        start=True, stop=True,
                    )
                nc.vector.tensor_tensor(
                    out=shifted[:, n0:n1, :], in0=bank[:, 0 : n1 - n0, :], in1=road_sb[s][:, n0:n1, :], op=ALU.add
                )
            return shifted

        for s in range(SLICES):
            picked = gather_words(s)
            half_sin = work.tile([P, PACK, W], F32)
            sin_sq = work.tile([P, PACK, W], F32)
            gain_cos = work.tile([P, PACK, W], F32)
            tanh = work.tile([P, PACK, W], F32, bufs=3)
            for pair in range(2):
                e2 = first_stage_bank(1, pair, picked, s)
                nc.scalar.activation(out=half_sin[:, 2 * pair : 2 * pair + 2, :], in_=e2[:], func=ACT.Sin, scale=0.5)
            for pair in range(2):
                both = slice(2 * pair, 2 * pair + 2)
                nc.scalar.activation(out=sin_sq[:, both, :], in_=half_sin[:, both, :], func=ACT.Square)
            for t in range(PACK):
                nc.scalar.activation(
                    out=gain_cos[:, t, :], in_=sin_sq[:, t, :], func=ACT.Identity,
                    scale=gain_m2[:, t : t + 1], bias=gain_sb[:, t : t + 1],
                )
            for pair in range(2):
                e1 = first_stage_bank(0, pair, picked, s)
                nc.scalar.activation(out=tanh[:, 2 * pair : 2 * pair + 2, :], in_=e1[:], func=ACT.Tanh)
            if s > 0:
                shifted = second_stage(s - 1, h_codes, h_scales)

            h_bf = work.tile([P, PACK * W], BF16, align_bytes=64)
            nc.vector.tensor_tensor(
                out=h_bf[:].rearrange("p (c i t) -> p c t i", i=2, t=PACK),
                in0=gain_cos[:].rearrange("p t (c i) -> p c t i", i=2),
                in1=tanh[:].rearrange("p t (c i) -> p c t i", i=2),
                op=ALU.mult,
            )
            last = s == SLICES - 1
            if last:
                spots = [gain_cos[:, 0, :], tanh[:, 0, :], tanh[:, 2, :]]
            else:
                spots = [tanh[:, n, :] for n in range(ROW_TILES)]
            if s > 0:
                for n in range(ROW_TILES):
                    nc.scalar.activation(out=spots[n], in_=shifted[:, n, :], func=ACT.Abs)
            h_codes = work.tile([P, W], U32, align_bytes=64)
            h_scales = work.tile([P, W], U8, align_bytes=64)
            nc.vector.quantize_mx(out=h_codes[:].bitcast(FP8X4), scales=h_scales[:], in_=h_bf[:])
            if s > 0:
                for n in range(1 if last else ROW_TILES):
                    place(n, spots[n], (s - 1) * W, W)

        shifted = second_stage(SLICES - 1, h_codes, h_scales)
        spots = [gain_cos[:, 1, :], tanh[:, 1, :], tanh[:, 3, :]]
        for n in range(ROW_TILES):
            nc.scalar.activation(out=spots[n], in_=shifted[:, n, :], func=ACT.Abs)
        place(0, spots[0], S - W, W)
        for n in range(1, ROW_TILES):
            place(n, tanh[:, 2 * n - 2 : 2 * n, :].rearrange("p u j -> p (u j)"), S - 2 * W, 2 * W)

        for n in range(ROW_TILES):
            nc.sync.dma_start(out=out[P * n : P * (n + 1), :], in_=pages[n][:])
